import numpy as np
import ml_dtypes


def mxq(x, axis, fmt="e4m3"):
    dtype, down = {"e4m3": (ml_dtypes.float8_e4m3fn, 7), "e5m2": (ml_dtypes.float8_e5m2, 14)}[fmt]
    v = np.moveaxis(np.asarray(x, np.float32).astype(ml_dtypes.bfloat16).astype(np.float64), axis, -1)
    blocks = v.reshape(v.shape[:-1] + (-1, 32))
    amax = np.abs(blocks).max(-1, keepdims=True)
    byte = np.maximum(np.where(amax > 0, np.frexp(amax)[1] - 1 + 127, 0) - down, 1)
    scale = np.exp2(byte - 127.0)
    codes = (blocks / scale).astype(np.float32).astype(dtype).astype(np.float64)
    return np.moveaxis((codes * scale).reshape(v.shape), -1, axis)


WIDE = False


def mx_kscale(k):
    if not WIDE:
        return np.ones(k)
    levels = np.array([10, -10, 5, -5, 0])
    if k % 512:
        return np.exp2(np.random.permutation(np.resize(levels, k // 32))).repeat(32)
    a = np.empty((k // 512, 16))
    for p in range(k // 512):
        a[p, :8] = np.random.permutation(np.resize(levels, 8))
        for g in range(8):
            far = levels[np.abs(levels - a[p, g]) >= 10]
            a[p, g + 8] = far[np.random.randint(len(far))]
    return np.exp2(a.ravel()).repeat(32)


def f64(x):
    return np.asarray(x).astype(np.float64)


def striped(idx):
    return np.tile(idx.reshape(-1, 16).T, (8, 1)).astype(np.uint16)


def unstriped(offs):
    return offs[:16].T.reshape(-1).astype(np.int64)


E2M1 = np.array([0.0, 0.5, 1.0, 1.5, 2.0, 3.0, 4.0, 6.0, -0.0, -0.5, -1.0, -1.5, -2.0, -3.0, -4.0, -6.0])


def pack_weight(w, fmt):
    k, n = w.shape
    w = f64(np.asarray(w, np.float32).astype(ml_dtypes.bfloat16)).reshape(k // 32, 32, n)
    amax = np.abs(w).max(1)
    if fmt == "e4m3":
        byte = np.frexp(amax)[1] - 1 + 127 - 7
    else:
        mant, ex = np.frexp(amax / 6.0)
        byte = np.where(mant > 0.5, ex, ex - 1) + 127
    byte = np.clip(np.where(amax > 0, byte, 1), 1, 254)
    scaled = (w * np.exp2(127.0 - byte)[:, None, :]).reshape(k, n).astype(np.float32)
    by_word = np.ascontiguousarray(scaled.reshape(k // 512, 128, 4, n).transpose(0, 1, 3, 2))
    if fmt == "e4m3":
        words = by_word.astype(ml_dtypes.float8_e4m3fn).view(np.uint8)
    else:
        c = by_word.astype(ml_dtypes.float4_e2m1fn).view(np.uint8) & 0xF
        words = (c[..., 0::2] | (c[..., 1::2] << 4)).reshape(k // 512, 128, 2 * n)
    return np.ascontiguousarray(words), np.ascontiguousarray(byte.astype(np.uint8).reshape(k // 512, 16, n))


def unpack_weight(words, scales, fmt):
    g, _, n = scales.shape
    words = np.ascontiguousarray(words).reshape(g, 128, n, -1)
    if fmt == "e4m3":
        vals = words.view(ml_dtypes.float8_e4m3fn).astype(np.float64)
    else:
        nib = np.empty((g, 128, n, 4), np.uint8)
        nib[..., 0::2] = words & 0xF
        nib[..., 1::2] = words >> 4
        vals = E2M1[nib]
    vals = vals * np.repeat(np.exp2(scales.astype(np.float64) - 127.0), 8, axis=1)[..., None]
    return vals.transpose(0, 1, 3, 2).reshape(g * 512, n)


def gelu(v):
    return 0.5 * v * (1.0 + np.tanh(np.sqrt(2.0 / np.pi) * (v + 0.044715 * v**3)))


K, H, T, S, P, T2 = 1536, 512, 4096, 1024, 1024, 2048


def setup_inputs():
    n = np.random.standard_normal
    s = mx_kscale(K)[:, None]
    u = mx_kscale(H)[:, None]
    d = {}
    d["tab_words"], d["tab_scales"] = pack_weight(n((K, T)) * s, "e4m3")
    d["offs"] = striped(np.random.permutation(T)[:S])
    d["offs2"] = striped(np.random.permutation(T2)[:S])
    d["offs3"] = striped(np.random.permutation(T2)[:P])
    d["offs4"] = striped(np.random.permutation(T2)[:P])
    d["w4_words"], d["w4_scales"] = pack_weight(1.4 * n((K, H)) / K**0.5 / s, "e2m1")
    d["gain"] = (np.exp(0.3 * n(H)) * u[:, 0]).astype(np.float32)
    d["wgs"] = np.exp(0.3 * n((128, S))).astype(np.float32)
    d["page0"] = (n((H, T2)) * u).astype(np.float32)
    d["gm"] = n((H, P)).astype(np.float32)
    d["w2"] = (1.3 * n((H, H)) / H**0.5 / u).astype(np.float32)
    d["back"] = (np.exp(0.3 * n(H)) / u[:, 0]).astype(np.float32)
    d["wgo"] = np.exp(0.3 * n((128, P))).astype(np.float32)
    d["page1"] = n((H, T2)).astype(np.float32)
    return d


def reference(tab_words, tab_scales, offs, offs2, offs3, offs4, w4_words, w4_scales,
              gain, wgs, page0, gm, w2, back, wgo, page1):
    v = unpack_weight(tab_words, tab_scales, "e4m3")[:, unstriped(offs)]
    w4 = unpack_weight(w4_words, w4_scales, "e2m1")
    a = w4.T @ v
    h = 0.5 * a * (1.0 + np.tanh(0.7978845608028654 * (a + 0.044715 * a**3))) * f64(gain)[:, None]
    page = f64(page0).copy()
    page[:, unstriped(offs2)] = np.tile(f64(wgs), (H // 128, 1)) * h
    x = page[:, unstriped(offs3)]
    xm = mxq(x * f64(gm), 0, "e4m3")
    y = np.tanh(mxq(f64(w2), 0, "e4m3").T @ xm)
    y = y + f64(back)[:, None] * x
    out = f64(page1).copy()
    out[:, unstriped(offs4)] = np.tile(f64(wgo), (H // 128, 1)) * y
    return out

@@ -1,0 +1,295 @@
+from contextlib import ExitStack
+
+import concourse.mybir as mybir
+
+K, H, T, S, T2 = 1536, 512, 4096, 1024, 2048
+FLOPS = 2 * K * H * S + 2 * H * H * S
+
+F32 = mybir.dt.float32
+BF16 = mybir.dt.bfloat16
+I32 = mybir.dt.int32
+U32 = mybir.dt.uint32
+U16 = mybir.dt.uint16
+U8 = mybir.dt.uint8
+FP8X4 = mybir.dt.float8_e4m3fn_x4
+FP4X4 = mybir.dt.float4_e2m1fn_x4
+ACT = mybir.ActivationFunctionType
+MULT = mybir.AluOpType.mult
+ADD = mybir.AluOpType.add
+
+P = 128
+PACK = 4
+PASSES = K // (P * PACK)
+HALF = S // 2
+LIST_COLS = S // 16
+
+
+def tile_list_toll_class_page_kernel(
+    tc, tab_words, tab_scales, offs, offs2, offs3, offs4, w4_words, w4_scales,
+    gain, wgs, page0, gm, w2, back, wgo, page1, out,
+):
+    nc = tc.nc
+    with ExitStack() as ctx:
+        lists = ctx.enter_context(tc.tile_pool(name="lists", bufs=1))
+        keep = ctx.enter_context(tc.tile_pool(name="keep", bufs=1))
+        psum = ctx.enter_context(tc.psum_pool(name="psum", bufs=1))
+
+        def cols(h):
+            return slice(h * HALF, (h + 1) * HALF)
+
+        def list_half(tile, h):
+            return tile[:, h * LIST_COLS // 2:(h + 1) * LIST_COLS // 2]
+
+        def rows_of(ap, t):
+            return ap.rearrange("(p t) c -> p t c", t=PACK)[:, t, :]
+
+        idx1 = lists.tile([P, LIST_COLS], U16, name="idx1")
+        idx2 = lists.tile([P, LIST_COLS], U16, name="idx2")
+        idx3 = lists.tile([P, LIST_COLS], U16, name="idx3")
+        idx4 = lists.tile([P, LIST_COLS], U16, name="idx4")
+
+        tab_sc = keep.tile([P, T], U8, name="tab_sc", align_bytes=64)
+        nc.vector.memset(tab_sc[0:48, :].bitcast(I32), 0)
+        nc.vector.memset(tab_sc[96:128, :].bitcast(I32), 0)
+        w4_sc_raw = keep.tile([P, PASSES * H], U8, name="w4_sc_raw", align_bytes=64)
+        nc.vector.memset(w4_sc_raw[:].bitcast(I32), 0)
+        v_planes = keep.tile([P, PASSES * S], U8, name="v_planes", align_bytes=64)
+        nc.vector.memset(v_planes[:].bitcast(I32), 0)
+
+        nc.sync.dma_start(idx1[:], offs)
+        w4_raw = keep.tile([P, PASSES * 2 * H], U8, name="w4_raw", align_bytes=64)
+        nc.sync.dma_start(
+            w4_raw[:].bitcast(I32).rearrange("p (a w) -> p a w", a=PASSES),
+            w4_words.bitcast(I32).rearrange("a p w -> p a w"),
+        )
+        nc.sync.dma_start(
+            tab_sc[48:96, :].bitcast(I32),
+            tab_scales.bitcast(I32).rearrange("a q w -> q a w"),
+        )
+        tab_w = [keep.tile([P, T], U32, name=f"tab_w{a}", tag="big", bufs=3, align_bytes=64) for a in range(PASSES)]
+
+        def load_tab(a):
+            nc.sync.dma_start(
+                tab_w[a][:].bitcast(I32),
+                tab_words[a].rearrange("p t i -> p (t i)").bitcast(I32),
+            )
+
+        load_tab(0)
+        load_tab(1)
+        for Q in range(4):
+            nc.gpsimd.dma_start(
+                w4_sc_raw[32 * Q:32 * Q + 4, :].bitcast(I32).rearrange("r (a w) -> r a w", a=PASSES),
+                w4_scales.bitcast(I32)[:, 4 * Q:4 * Q + 4, :].rearrange("a r w -> r a w"),
+            )
+        gain_sb = keep.tile([P, PACK], F32, name="gain_sb")
+        nc.gpsimd.dma_start(gain_sb[:], gain.rearrange("(p t) -> p t", t=PACK))
+        back_sb = keep.tile([P, PACK], F32, name="back_sb")
+        nc.gpsimd.dma_start(back_sb[:], back.rearrange("(p t) -> p t", t=PACK))
+
+        wgs_first = keep.tile([P, S], F32, name="wgs_first", tag="first")
+        wgs_rest = keep.tile([P, PACK - 1, S], F32, name="wgs_rest", tag="rest")
+        gained = keep.tile([P, PACK, S], F32, name="gained")
+        wgs_rows = wgs.rearrange("(q t) j -> q t j", t=PACK)
+        for Q in (0, 2, 1, 3):
+            nc.sync.dma_start(wgs_first[32 * Q:32 * Q + 32, :], wgs_rows[:, 0, :])
+        load_tab(2)
+        nc.sync.dma_start(idx2[:], offs2)
+        page0_sb = [keep.tile([P, T2], F32, name=f"page0_{t}") for t in range(PACK)]
+        nc.sync.dma_start(page0_sb[0][:], rows_of(page0, 0))
+        for Q in (0, 2, 1, 3):
+            nc.sync.dma_start(wgs_rest[32 * Q:32 * Q + 32, :, :], wgs_rows[:, 1:PACK, :])
+        nc.sync.dma_start(page0_sb[1][:], rows_of(page0, 1))
+        nc.sync.dma_start(idx3[:], offs3)
+
+        def wgs_of(t):
+            return gained[:, t, :]
+
+        picked_sc = keep.tile([P, S], U8, name="picked_sc", align_bytes=64)
+        nc.vector.tensor_copy(picked_sc[:], tab_sc[:].indirect(idx1[:]))
+        for Q in range(4):
+            nc.scalar.dma_start(
+                v_planes[32 * Q:32 * Q + 4, :].bitcast(I32),
+                picked_sc[48 + 12 * Q:60 + 12 * Q, :].bitcast(I32),
+            )
+        w4_codes = keep.tile([P, PASSES * 2 * H], U8, name="w4_codes", align_bytes=64)
+        nc.vector.tensor_copy(
+            w4_codes[:].rearrange("p (a t q b) -> p a t q b", a=PASSES, t=PACK, b=2),
+            w4_raw[:].rearrange("p (a q t b) -> p a t q b", a=PASSES, t=PACK, b=2),
+        )
+        v_words = [keep.tile([P, S], U32, name=f"v_words{a}", align_bytes=64) for a in range(PASSES)]
+        nc.vector.tensor_copy(v_words[0][:], tab_w[0][:].indirect(idx1[:]))
+        w4_planes = keep.tile([P, PASSES * H], U8, name="w4_planes", align_bytes=64)
+        nc.vector.tensor_copy(
+            w4_planes[:].rearrange("p (a t q) -> p a t q", a=PASSES, t=PACK),
+            w4_sc_raw[:].rearrange("p (a q t) -> p a t q", a=PASSES, t=PACK),
+        )
+        nc.vector.tensor_copy(v_words[1][:], tab_w[1][:].indirect(idx1[:]))
+        for h in range(2):
+            nc.vector.tensor_copy(v_words[2][:, cols(h)], tab_w[2][:].indirect(list_half(idx1, h)))
+
+        gm_sb = keep.tile([P, PACK, S], F32, name="gm_sb")
+        nc.sync.dma_start(gm_sb[:], gm.rearrange("(p t) j -> p t j", t=PACK))
+        nc.sync.dma_start(page0_sb[2][:], rows_of(page0, 2))
+        wgo_sb = keep.tile([P, PACK, S], F32, name="wgo_sb", tag="big", bufs=3, align_bytes=64)
+        w2_raw = keep.tile([P, PACK, H], F32, name="w2_raw")
+        page1_sb = [keep.tile([P, T2], F32, name=f"page1_{t}", tag="big", bufs=3, align_bytes=64) for t in range(2)]
+        page1_sb.extend([keep.tile([P, T2], F32, name=f"page1_{t}") for t in range(2, PACK)])
+        nc.sync.dma_start(w2_raw[:], w2.rearrange("(p j) n -> p j n", j=PACK))
+        nc.sync.dma_start(page0_sb[3][:], rows_of(page0, 3))
+        nc.sync.dma_start(idx4[:], offs4)
+        wgo_rows = wgo.rearrange("(q t) j -> q t j", t=PACK)
+        for Q in (0, 2, 1, 3):
+            nc.sync.dma_start(wgo_sb[32 * Q:32 * Q + 32, :, :], wgo_rows)
+        for t in range(PACK):
+            nc.sync.dma_start(page1_sb[t][:], rows_of(page1, t))
+
+        h_sb = []
+
+        def first_product(t, ht):
+            for h in range(2):
+                acc = psum.tile([P, HALF], F32, name="acc1", tag="acc1", bufs=2)
+                for a in range(PASSES):
+                    nc.tensor.matmul_mx(
+                        out=acc[:],
+                        lhsT=w4_codes[:, (a * PACK + t) * 2 * P:(a * PACK + t + 1) * 2 * P].bitcast(FP4X4),
+                        lhsT_scale=w4_planes[:, (a * PACK + t) * P:(a * PACK + t + 1) * P],
+                        rhs=v_words[a][:, cols(h)].bitcast(FP8X4),
+                        rhs_scale=v_planes[:, a * S + h * HALF:a * S + (h + 1) * HALF],
+                        start=(a == 0),
+                        stop=(a == PASSES - 1),
+                    )
+                nc.scalar.activation(ht[:, cols(h)], acc[:], ACT.Gelu_apprx_tanh)
+            h_sb.append(ht)
+
+        def put_states(t, h):
+            if h is None:
+                nc.vector.tensor_tensor(page0_sb[t][:].indirect(idx2[:]), h_sb[t], wgs_of(t), MULT)
+            else:
+                nc.vector.tensor_tensor(
+                    page0_sb[t][:].indirect(list_half(idx2, h)), h_sb[t][:, cols(h)], wgs_of(t)[:, cols(h)], MULT)
+
+        x_sb = {}
+        prod = {0: keep.tile([P, PACK, HALF], BF16, name="prod0")}
+        woven = [keep.tile([P, HALF, PACK], BF16, name=f"woven{h}", tag=f"woven{h}", align_bytes=64) for h in range(2)]
+        x_codes = [keep.tile([P, HALF], U32, name=f"x_codes{h}", align_bytes=64) for h in range(2)]
+        x_planes = [keep.tile([P, HALF], U8, name=f"x_planes{h}", align_bytes=64) for h in range(2)]
+
+        def recall(t, h):
+            nc.vector.tensor_copy(x_sb[h][:, t, :], page0_sb[t][:].indirect(list_half(idx3, h)))
+
+        def weigh(t, h):
+            nc.vector.tensor_tensor(prod[h][:, t, :], x_sb[h][:, t, :], gm_sb[:, t, cols(h)], MULT)
+
+        def weave(h):
+            nc.scalar.copy(
+                woven[h][:].rearrange("p (c i) t -> p c t i", i=4),
+                prod[h][:].rearrange("p t (c i) -> p c t i", i=4),
+            )
+
+        def quantise(h):
+            nc.vector.quantize_mx(
+                out=x_codes[h][:].bitcast(FP8X4), scales=x_planes[h][:],
+                in_=woven[h][:].rearrange("p j t -> p (j t)"),
+            )
+
+        w2_woven = keep.tile([P, PACK * H], BF16, name="w2_woven", align_bytes=64)
+        w2_codes = keep.tile([P, H], U32, name="w2_codes", align_bytes=64)
+        w2_planes = keep.tile([P, H], U8, name="w2_planes", align_bytes=64)
+
+        x_sb[0] = keep.tile([P, PACK, HALF], F32, name="x_first")
+        nc.scalar.activation(wgs_of(0), wgs_first[:], ACT.Copy, scale=gain_sb[:, 0:1])
+        h_first = keep.tile([P, S], F32, name="h_first", tag="first")
+        first_product(0, h_first[:])
+        put_states(0, 0)
+        put_states(0, 1)
+        for t in range(1, PACK):
+            nc.scalar.activation(wgs_of(t), wgs_rest[:, t - 1, :], ACT.Copy, scale=gain_sb[:, t:t + 1])
+        h_rest = keep.tile([P, PACK - 1, S], F32, name="h_rest", tag="rest")
+        first_product(1, h_rest[:, 0, :])
+        put_states(1, None)
+        recall(0, 0)
+        first_product(2, h_rest[:, 1, :])
+        put_states(2, None)
+        weigh(0, 0)
+        recall(1, 0)
+        first_product(3, h_rest[:, 2, :])
+        nc.scalar.copy(
+            w2_woven[:].rearrange("p (t m j) -> p t m j", t=PACK, j=PACK),
+            w2_raw[:].rearrange("p j (m t) -> p t m j", t=PACK),
+        )
+        put_states(3, None)
+        x_sb[1] = keep.tile([P, PACK, HALF], F32, name="x_second", tag="rest")
+        weigh(1, 0)
+        recall(2, 0)
+        recall(3, 0)
+        weigh(2, 0)
+        nc.vector.quantize_mx(out=w2_codes[:].bitcast(FP8X4), scales=w2_planes[:], in_=w2_woven[:])
+        weigh(3, 0)
+        weave(0)
+        for t in range(PACK):
+            recall(t, 1)
+        quantise(0)
+        prod[1] = keep.tile([P, PACK, HALF], BF16, name="prod1", tag="woven0", align_bytes=64)
+        for t in range(PACK):
+            weigh(t, 1)
+
+        y_sb = [keep.tile([P, S], F32, name=f"y{t}", tag="y", bufs=4) for t in range(PACK)]
+        y_in = {}
+
+        def second_product(t, h):
+            acc = psum.tile([P, HALF], F32, name="acc2", tag="acc2", bufs=4)
+            nc.tensor.matmul_mx(
+                out=acc[:],
+                lhsT=w2_codes[:, t * P:(t + 1) * P].bitcast(FP8X4),
+                lhsT_scale=w2_planes[:, t * P:(t + 1) * P],
+                rhs=x_codes[h][:].bitcast(FP8X4),
+                rhs_scale=x_planes[h][:],
+                start=True,
+                stop=True,
+            )
+            nc.scalar.activation(y_sb[t][:, cols(h)], acc[:], ACT.Tanh)
+
+        def add_recalled(t, h):
+            nc.vector.scalar_tensor_tensor(
+                y_in.get((t, h), y_sb[t][:, cols(h)]), x_sb[h][:, t, :], back_sb[:, t:t + 1], y_sb[t][:, cols(h)], MULT, ADD)
+
+        def put_result(t, h):
+            if h is None:
+                nc.vector.tensor_tensor(page1_sb[t][:].indirect(idx4[:]), y_sb[t][:], wgo_sb[:, t, :], MULT)
+            else:
+                nc.vector.tensor_tensor(
+                    page1_sb[t][:].indirect(list_half(idx4, h)), y_in.get((t, h), y_sb[t][:, cols(h)]), wgo_sb[:, t, cols(h)], MULT)
+
+        def store(t):
+            nc.sync.dma_start(rows_of(out, t), page1_sb[t][:])
+
+        second_product(0, 0)
+        second_product(1, 0)
+        weave(1)
+        add_recalled(0, 0)
+        put_result(0, 0)
+        quantise(1)
+        y_held = keep.tile([P, HALF], F32, name="y_held", tag="woven1", align_bytes=64)
+        y_in[(1, 0)] = y_held[:]
+        second_product(0, 1)
+        second_product(1, 1)
+        for t in (2, 3):
+            second_product(t, 0)
+            second_product(t, 1)
+        add_recalled(1, 0)
+        put_result(1, 0)
+        add_recalled(0, 1)
+        add_recalled(1, 1)
+        put_result(0, 1)
+        store(0)
+        for t in (2, 3):
+            add_recalled(t, 0)
+            add_recalled(t, 1)
+            if t == 2:
+                put_result(1, 1)
+                store(1)
+            else:
+                put_result(2, None)
+                store(2)
+        put_result(3, None)
+        store(3)

@@ -1,6 +1,7 @@
 from contextlib import ExitStack
 
 import concourse.mybir as mybir
+from concourse.masks import make_identity
 
 K, H, T, S, T2 = 1536, 512, 4096, 1024, 2048
 FLOPS = 2 * K * H * S + 2 * H * H * S
@@ -22,6 +23,9 @@ PACK = 4
 PASSES = K // (P * PACK)
 HALF = S // 2
 LIST_COLS = S // 16
+ROWS = 16 * PASSES
+ROW0 = 48
+PLANE = S + H
 
 
 def tile_list_toll_class_page_kernel(
@@ -49,22 +53,29 @@ def tile_list_toll_class_page_kernel(
         idx4 = lists.tile([P, LIST_COLS], U16, name="idx4")
 
         tab_sc = keep.tile([P, T], U8, name="tab_sc", align_bytes=64)
-        nc.vector.memset(tab_sc[0:48, :].bitcast(I32), 0)
-        nc.vector.memset(tab_sc[96:128, :].bitcast(I32), 0)
-        w4_sc_raw = keep.tile([P, PASSES * H], U8, name="w4_sc_raw", align_bytes=64)
-        nc.vector.memset(w4_sc_raw[:].bitcast(I32), 0)
-        v_planes = keep.tile([P, PASSES * S], U8, name="v_planes", align_bytes=64)
-        nc.vector.memset(v_planes[:].bitcast(I32), 0)
+        w4_sc = keep.tile([P, H], U8, name="w4_sc", align_bytes=64)
+        for tile in (tab_sc, w4_sc):
+            nc.vector.memset(tile[0:ROW0, :].bitcast(I32), 0)
+            nc.vector.memset(tile[ROW0 + ROWS:P, :].bitcast(I32), 0)
+        planes = keep.tile([P, PASSES * PLANE], U8, name="planes", align_bytes=64)
+        nc.gpsimd.memset(planes[:].bitcast(I32), 0)
+        gain_sb = keep.tile([P, PACK], F32, name="gain_sb")
+        nc.gpsimd.dma_start(gain_sb[:], gain.rearrange("(p t) -> p t", t=PACK))
+        back_sb = keep.tile([P, PACK], F32, name="back_sb")
+        nc.gpsimd.dma_start(back_sb[:], back.rearrange("(p t) -> p t", t=PACK))
+        ident = keep.tile([P, P], F32, name="ident")
+        make_identity(nc, ident[:])
 
         nc.sync.dma_start(idx1[:], offs)
+        for tile, rows in ((tab_sc, tab_scales), (w4_sc, w4_scales)):
+            nc.scalar.dma_start(
+                tile[ROW0:ROW0 + ROWS, :].bitcast(I32),
+                rows.bitcast(I32).rearrange("a q w -> q a w"),
+            )
         w4_raw = keep.tile([P, PASSES * 2 * H], U8, name="w4_raw", align_bytes=64)
-        nc.sync.dma_start(
+        nc.scalar.dma_start(
             w4_raw[:].bitcast(I32).rearrange("p (a w) -> p a w", a=PASSES),
             w4_words.bitcast(I32).rearrange("a p w -> p a w"),
-        )
-        nc.sync.dma_start(
-            tab_sc[48:96, :].bitcast(I32),
-            tab_scales.bitcast(I32).rearrange("a q w -> q a w"),
         )
         tab_w = [keep.tile([P, T], U32, name=f"tab_w{a}", tag="big", bufs=3, align_bytes=64) for a in range(PASSES)]
 
@@ -74,87 +85,89 @@ def tile_list_toll_class_page_kernel(
                 tab_words[a].rearrange("p t i -> p (t i)").bitcast(I32),
             )
 
-        load_tab(0)
-        load_tab(1)
-        for Q in range(4):
-            nc.gpsimd.dma_start(
-                w4_sc_raw[32 * Q:32 * Q + 4, :].bitcast(I32).rearrange("r (a w) -> r a w", a=PASSES),
-                w4_scales.bitcast(I32)[:, 4 * Q:4 * Q + 4, :].rearrange("a r w -> r a w"),
-            )
-        gain_sb = keep.tile([P, PACK], F32, name="gain_sb")
-        nc.gpsimd.dma_start(gain_sb[:], gain.rearrange("(p t) -> p t", t=PACK))
-        back_sb = keep.tile([P, PACK], F32, name="back_sb")
-        nc.gpsimd.dma_start(back_sb[:], back.rearrange("(p t) -> p t", t=PACK))
+        def load_dealt(dst, src):
+            for Q in (0, 2, 1, 3):
+                nc.sync.dma_start(dst[32 * Q:32 * Q + 32], src)
 
-        wgs_first = keep.tile([P, S], F32, name="wgs_first", tag="first")
-        wgs_rest = keep.tile([P, PACK - 1, S], F32, name="wgs_rest", tag="rest")
+        wgs_raw = [keep.tile([P, S], F32, name=f"wgs_raw{t}", tag=f"h{t}") for t in range(PACK)]
         gained = keep.tile([P, PACK, S], F32, name="gained")
         wgs_rows = wgs.rearrange("(q t) j -> q t j", t=PACK)
-        for Q in (0, 2, 1, 3):
-            nc.sync.dma_start(wgs_first[32 * Q:32 * Q + 32, :], wgs_rows[:, 0, :])
+        page0_sb = [keep.tile([P, T2], F32, name=f"page0_{t}") for t in range(PACK)]
+
+        load_tab(0)
+        load_tab(1)
         load_tab(2)
         nc.sync.dma_start(idx2[:], offs2)
-        page0_sb = [keep.tile([P, T2], F32, name=f"page0_{t}") for t in range(PACK)]
+        load_dealt(wgs_raw[0][:, cols(0)], wgs_rows[:, 0, cols(0)])
         nc.sync.dma_start(page0_sb[0][:], rows_of(page0, 0))
-        for Q in (0, 2, 1, 3):
-            nc.sync.dma_start(wgs_rest[32 * Q:32 * Q + 32, :, :], wgs_rows[:, 1:PACK, :])
+        load_dealt(wgs_raw[0][:, cols(1)], wgs_rows[:, 0, cols(1)])
+        load_dealt(wgs_raw[1][:], wgs_rows[:, 1, :])
         nc.sync.dma_start(page0_sb[1][:], rows_of(page0, 1))
         nc.sync.dma_start(idx3[:], offs3)
-
-        def wgs_of(t):
-            return gained[:, t, :]
+        load_dealt(wgs_raw[2][:], wgs_rows[:, 2, :])
+        nc.sync.dma_start(page0_sb[2][:], rows_of(page0, 2))
+        gm_sb = keep.tile([P, PACK, S], F32, name="gm_sb")
+        nc.sync.dma_start(gm_sb[:], gm.rearrange("(p t) j -> p t j", t=PACK))
+        load_dealt(wgs_raw[3][:], wgs_rows[:, 3, :])
+        nc.sync.dma_start(page0_sb[3][:], rows_of(page0, 3))
+        w2_raw = keep.tile([P, PACK, H], F32, name="w2_raw", tag="w2_raw")
+        nc.sync.dma_start(w2_raw[:], w2.rearrange("(p j) n -> p j n", j=PACK))
+        nc.sync.dma_start(idx4[:], offs4)
 
         picked_sc = keep.tile([P, S], U8, name="picked_sc", align_bytes=64)
         nc.vector.tensor_copy(picked_sc[:], tab_sc[:].indirect(idx1[:]))
+        staged = keep.tile([P, PLANE], U8, name="staged", align_bytes=64)
+        nc.vector.tensor_copy(
+            staged[:, S:PLANE].rearrange("p (t q) -> p t q", t=PACK),
+            w4_sc[:].rearrange("p (q t) -> p t q", t=PACK),
+        )
+        nc.vector.tensor_copy(staged[:, 0:S].bitcast(I32), picked_sc[:].bitcast(I32))
         for Q in range(4):
-            nc.scalar.dma_start(
-                v_planes[32 * Q:32 * Q + 4, :].bitcast(I32),
-                picked_sc[48 + 12 * Q:60 + 12 * Q, :].bitcast(I32),
+            first = ROW0 + 4 * PASSES * Q
+            nc.gpsimd.dma_start(
+                planes[32 * Q:32 * Q + 4, :].bitcast(I32),
+                staged[first:first + 4 * PASSES, :].bitcast(I32),
             )
         w4_codes = keep.tile([P, PASSES * 2 * H], U8, name="w4_codes", align_bytes=64)
         nc.vector.tensor_copy(
-            w4_codes[:].rearrange("p (a t q b) -> p a t q b", a=PASSES, t=PACK, b=2),
-            w4_raw[:].rearrange("p (a q t b) -> p a t q b", a=PASSES, t=PACK, b=2),
+            w4_codes[:].bitcast(U16).rearrange("p (a t q) -> p a t q", a=PASSES, t=PACK),
+            w4_raw[:].bitcast(U16).rearrange("p (a q t) -> p a t q", a=PASSES, t=PACK),
         )
         v_words = [keep.tile([P, S], U32, name=f"v_words{a}", align_bytes=64) for a in range(PASSES)]
         nc.vector.tensor_copy(v_words[0][:], tab_w[0][:].indirect(idx1[:]))
-        w4_planes = keep.tile([P, PASSES * H], U8, name="w4_planes", align_bytes=64)
-        nc.vector.tensor_copy(
-            w4_planes[:].rearrange("p (a t q) -> p a t q", a=PASSES, t=PACK),
-            w4_sc_raw[:].rearrange("p (a q t) -> p a t q", a=PASSES, t=PACK),
-        )
         nc.vector.tensor_copy(v_words[1][:], tab_w[1][:].indirect(idx1[:]))
         for h in range(2):
             nc.vector.tensor_copy(v_words[2][:, cols(h)], tab_w[2][:].indirect(list_half(idx1, h)))
 
-        gm_sb = keep.tile([P, PACK, S], F32, name="gm_sb")
-        nc.sync.dma_start(gm_sb[:], gm.rearrange("(p t) j -> p t j", t=PACK))
-        nc.sync.dma_start(page0_sb[2][:], rows_of(page0, 2))
         wgo_sb = keep.tile([P, PACK, S], F32, name="wgo_sb", tag="big", bufs=3, align_bytes=64)
-        w2_raw = keep.tile([P, PACK, H], F32, name="w2_raw")
         page1_sb = [keep.tile([P, T2], F32, name=f"page1_{t}", tag="big", bufs=3, align_bytes=64) for t in range(2)]
         page1_sb.extend([keep.tile([P, T2], F32, name=f"page1_{t}") for t in range(2, PACK)])
-        nc.sync.dma_start(w2_raw[:], w2.rearrange("(p j) n -> p j n", j=PACK))
-        nc.sync.dma_start(page0_sb[3][:], rows_of(page0, 3))
-        nc.sync.dma_start(idx4[:], offs4)
         wgo_rows = wgo.rearrange("(q t) j -> q t j", t=PACK)
-        for Q in (0, 2, 1, 3):
-            nc.sync.dma_start(wgo_sb[32 * Q:32 * Q + 32, :, :], wgo_rows)
+        load_dealt(wgo_sb[:, :, cols(0)], wgo_rows[:, :, cols(0)])
         for t in range(PACK):
             nc.sync.dma_start(page1_sb[t][:], rows_of(page1, t))
+        load_dealt(wgo_sb[:, :, cols(1)], wgo_rows[:, :, cols(1)])
 
         h_sb = []
 
-        def first_product(t, ht):
+        def first_product(t):
+            if t == 0:
+                for h in range(2):
+                    nc.scalar.activation(
+                        gained[:, t, cols(h)], wgs_raw[t][:, cols(h)], ACT.Copy, scale=gain_sb[:, t:t + 1])
+                ht = keep.tile([P, S], F32, name="h_first")
+            else:
+                nc.scalar.activation(gained[:, t, :], wgs_raw[t][:], ACT.Copy, scale=gain_sb[:, t:t + 1])
+                ht = keep.tile([P, S], F32, name=f"h{t}", tag=f"h{t}")
             for h in range(2):
                 acc = psum.tile([P, HALF], F32, name="acc1", tag="acc1", bufs=2)
                 for a in range(PASSES):
                     nc.tensor.matmul_mx(
                         out=acc[:],
                         lhsT=w4_codes[:, (a * PACK + t) * 2 * P:(a * PACK + t + 1) * 2 * P].bitcast(FP4X4),
-                        lhsT_scale=w4_planes[:, (a * PACK + t) * P:(a * PACK + t + 1) * P],
+                        lhsT_scale=planes[:, a * PLANE + S + t * P:a * PLANE + S + (t + 1) * P],
                         rhs=v_words[a][:, cols(h)].bitcast(FP8X4),
-                        rhs_scale=v_planes[:, a * S + h * HALF:a * S + (h + 1) * HALF],
+                        rhs_scale=planes[:, a * PLANE + h * HALF:a * PLANE + (h + 1) * HALF],
                         start=(a == 0),
                         stop=(a == PASSES - 1),
                     )
@@ -163,15 +176,15 @@ def tile_list_toll_class_page_kernel(
 
         def put_states(t, h):
             if h is None:
-                nc.vector.tensor_tensor(page0_sb[t][:].indirect(idx2[:]), h_sb[t], wgs_of(t), MULT)
+                nc.vector.tensor_tensor(page0_sb[t][:].indirect(idx2[:]), h_sb[t][:], gained[:, t, :], MULT)
             else:
                 nc.vector.tensor_tensor(
-                    page0_sb[t][:].indirect(list_half(idx2, h)), h_sb[t][:, cols(h)], wgs_of(t)[:, cols(h)], MULT)
+                    page0_sb[t][:].indirect(list_half(idx2, h)), h_sb[t][:, cols(h)], gained[:, t, cols(h)], MULT)
 
         x_sb = {}
-        prod = {0: keep.tile([P, PACK, HALF], BF16, name="prod0")}
-        woven = [keep.tile([P, HALF, PACK], BF16, name=f"woven{h}", tag=f"woven{h}", align_bytes=64) for h in range(2)]
-        x_codes = [keep.tile([P, HALF], U32, name=f"x_codes{h}", align_bytes=64) for h in range(2)]
+        prod = {0: keep.tile([P, PACK, HALF], BF16, name="prod0", tag="prod0", align_bytes=64)}
+        woven = {0: keep.tile([P, HALF, PACK], BF16, name="woven0", tag="woven0", align_bytes=64)}
+        x_codes = {0: keep.tile([P, HALF], U32, name="x_codes0", align_bytes=64)}
         x_planes = [keep.tile([P, HALF], U8, name=f"x_planes{h}", align_bytes=64) for h in range(2)]
 
         def recall(t, h):
@@ -180,11 +193,13 @@ def tile_list_toll_class_page_kernel(
         def weigh(t, h):
             nc.vector.tensor_tensor(prod[h][:, t, :], x_sb[h][:, t, :], gm_sb[:, t, cols(h)], MULT)
 
-        def weave(h):
-            nc.scalar.copy(
-                woven[h][:].rearrange("p (c i) t -> p c t i", i=4),
-                prod[h][:].rearrange("p t (c i) -> p c t i", i=4),
-            )
+        def weave(h, pieces):
+            width = HALF // pieces
+            for n in range(pieces):
+                nc.scalar.copy(
+                    woven[h][:, n * width:(n + 1) * width, :].rearrange("p (c i) t -> p c t i", i=4),
+                    prod[h][:, :, n * width:(n + 1) * width].rearrange("p t (c i) -> p c t i", i=4),
+                )
 
         def quantise(h):
             nc.vector.quantize_mx(
@@ -196,36 +211,31 @@ def tile_list_toll_class_page_kernel(
         w2_codes = keep.tile([P, H], U32, name="w2_codes", align_bytes=64)
         w2_planes = keep.tile([P, H], U8, name="w2_planes", align_bytes=64)
 
-        x_sb[0] = keep.tile([P, PACK, HALF], F32, name="x_first")
-        nc.scalar.activation(wgs_of(0), wgs_first[:], ACT.Copy, scale=gain_sb[:, 0:1])
-        h_first = keep.tile([P, S], F32, name="h_first", tag="first")
-        first_product(0, h_first[:])
+        x_sb[0] = keep.tile([P, PACK, HALF], F32, name="x_first", tag="x_first")
+        first_product(0)
         put_states(0, 0)
         put_states(0, 1)
-        for t in range(1, PACK):
-            nc.scalar.activation(wgs_of(t), wgs_rest[:, t - 1, :], ACT.Copy, scale=gain_sb[:, t:t + 1])
-        h_rest = keep.tile([P, PACK - 1, S], F32, name="h_rest", tag="rest")
-        first_product(1, h_rest[:, 0, :])
+        first_product(1)
         put_states(1, None)
         recall(0, 0)
-        first_product(2, h_rest[:, 1, :])
+        first_product(2)
         put_states(2, None)
-        weigh(0, 0)
         recall(1, 0)
-        first_product(3, h_rest[:, 2, :])
+        weigh(0, 0)
+        first_product(3)
         nc.scalar.copy(
             w2_woven[:].rearrange("p (t m j) -> p t m j", t=PACK, j=PACK),
             w2_raw[:].rearrange("p j (m t) -> p t m j", t=PACK),
         )
         put_states(3, None)
-        x_sb[1] = keep.tile([P, PACK, HALF], F32, name="x_second", tag="rest")
-        weigh(1, 0)
+        x_sb[1] = keep.tile([P, PACK, HALF], F32, name="x_second", tag="h3")
         recall(2, 0)
+        weigh(1, 0)
         recall(3, 0)
         weigh(2, 0)
         nc.vector.quantize_mx(out=w2_codes[:].bitcast(FP8X4), scales=w2_planes[:], in_=w2_woven[:])
         weigh(3, 0)
-        weave(0)
+        weave(0, 1)
         for t in range(PACK):
             recall(t, 1)
         quantise(0)
@@ -233,11 +243,10 @@ def tile_list_toll_class_page_kernel(
         for t in range(PACK):
             weigh(t, 1)
 
-        y_sb = [keep.tile([P, S], F32, name=f"y{t}", tag="y", bufs=4) for t in range(PACK)]
-        y_in = {}
+        scaled = {0: keep.tile([P, PACK, HALF], F32, name="scaled0", tag="w2_raw")}
 
         def second_product(t, h):
-            acc = psum.tile([P, HALF], F32, name="acc2", tag="acc2", bufs=4)
+            acc = psum.tile([P, HALF], F32, name="acc2", tag="acc2", bufs=3)
             nc.tensor.matmul_mx(
                 out=acc[:],
                 lhsT=w2_codes[:, t * P:(t + 1) * P].bitcast(FP8X4),
@@ -247,49 +256,50 @@ def tile_list_toll_class_page_kernel(
                 start=True,
                 stop=True,
             )
-            nc.scalar.activation(y_sb[t][:, cols(h)], acc[:], ACT.Tanh)
+            mixed = keep.tile([P, HALF], F32, name="mixed", tag="mixed", bufs=2)
+            nc.scalar.activation(mixed[:], acc[:], ACT.Tanh)
+            return mixed
 
-        def add_recalled(t, h):
-            nc.vector.scalar_tensor_tensor(
-                y_in.get((t, h), y_sb[t][:, cols(h)]), x_sb[h][:, t, :], back_sb[:, t:t + 1], y_sb[t][:, cols(h)], MULT, ADD)
+        def sum_on_vector(t, h):
+            mixed = second_product(t, h)
+            y = keep.tile([P, HALF], F32, name="y", tag="y", bufs=3)
+            nc.vector.scalar_tensor_tensor(y[:], x_sb[h][:, t, :], back_sb[:, t:t + 1], mixed[:], MULT, ADD)
+            return y
 
-        def put_result(t, h):
-            if h is None:
-                nc.vector.tensor_tensor(page1_sb[t][:].indirect(idx4[:]), y_sb[t][:], wgo_sb[:, t, :], MULT)
-            else:
-                nc.vector.tensor_tensor(
-                    page1_sb[t][:].indirect(list_half(idx4, h)), y_in.get((t, h), y_sb[t][:, cols(h)]), wgo_sb[:, t, cols(h)], MULT)
+        def sum_on_tensor(t, h, y=None):
+            blocks = HALF // P
+            nc.scalar.activation(scaled[h][:, t, :], x_sb[h][:, t, :], ACT.Copy, scale=back_sb[:, t:t + 1])
+            mixed = second_product(t, h)
+            turned = psum.tile([P, HALF], F32, name="turned", tag="acc1", bufs=2)
+            for n, term in enumerate((scaled[h][:, t, :], mixed[:])):
+                for b in range(blocks):
+                    nc.tensor.matmul(
+                        turned[:, b * P:(b + 1) * P], lhsT=term[:, b * P:(b + 1) * P], rhs=ident[:],
+                        is_transpose=True, start=(n == 0 and b == 0), stop=(n == 1 and b == blocks - 1),
+                    )
+            turned_sb = keep.tile([P, HALF], F32, name="turned_sb", tag="turned_sb", bufs=2)
+            nc.scalar.copy(turned_sb[:], turned[:])
+            upright = psum.tile([P, HALF], F32, name="upright", tag="upright", bufs=3)
+            for b in range(blocks):
+                nc.tensor.transpose(upright[:, b * P:(b + 1) * P], turned_sb[:, b * P:(b + 1) * P], ident[:])
+            if y is None:
+                y = keep.tile([P, HALF], F32, name="y", tag="y", bufs=3)
+            nc.scalar.copy(y[:], upright[:])
+            return y
 
-        def store(t):
-            nc.sync.dma_start(rows_of(out, t), page1_sb[t][:])
+        def put_result(t, h, y):
+            nc.vector.tensor_tensor(page1_sb[t][:].indirect(list_half(idx4, h)), y[:], wgo_sb[:, t, cols(h)], MULT)
 
-        second_product(0, 0)
-        second_product(1, 0)
-        weave(1)
-        add_recalled(0, 0)
-        put_result(0, 0)
+        put_result(0, 0, sum_on_vector(0, 0))
+        y = sum_on_tensor(1, 0, keep.tile([P, HALF], F32, name="y_held", tag="held", align_bytes=64))
+        woven[1] = keep.tile([P, HALF, PACK], BF16, name="woven1", tag="prod0", align_bytes=64)
+        weave(1, 4)
+        put_result(1, 0, y)
+        x_codes[1] = keep.tile([P, HALF], U32, name="x_codes1", tag="held", align_bytes=64)
         quantise(1)
-        y_held = keep.tile([P, HALF], F32, name="y_held", tag="woven1", align_bytes=64)
-        y_in[(1, 0)] = y_held[:]
-        second_product(0, 1)
-        second_product(1, 1)
-        for t in (2, 3):
-            second_product(t, 0)
-            second_product(t, 1)
-        add_recalled(1, 0)
-        put_result(1, 0)
-        add_recalled(0, 1)
-        add_recalled(1, 1)
-        put_result(0, 1)
-        store(0)
-        for t in (2, 3):
-            add_recalled(t, 0)
-            add_recalled(t, 1)
-            if t == 2:
-                put_result(1, 1)
-                store(1)
-            else:
-                put_result(2, None)
-                store(2)
-        put_result(3, None)
-        store(3)
+        for t in range(2, PACK):
+            put_result(t, 0, sum_on_tensor(t, 0))
+        scaled[1] = keep.tile([P, PACK, HALF], F32, name="scaled1", tag="x_first")
+        for t in range(PACK):
+            put_result(t, 1, sum_on_tensor(t, 1))
+            nc.sync.dma_start(rows_of(out, t), page1_sb[t][:])

@@ -197,8 +197,8 @@ def tile_list_toll_class_page_kernel(
             width = HALF // pieces
             for n in range(pieces):
                 nc.scalar.copy(
-                    woven[h][:, n * width:(n + 1) * width, :].rearrange("p (c i) t -> p c t i", i=4),
-                    prod[h][:, :, n * width:(n + 1) * width].rearrange("p t (c i) -> p c t i", i=4),
+                    woven[h][:, n * width:(n + 1) * width, :],
+                    prod[h][:, :, n * width:(n + 1) * width].rearrange("p t j -> p j t"),
                 )
 
         def quantise(h):
@@ -240,8 +240,7 @@ def tile_list_toll_class_page_kernel(
             recall(t, 1)
         quantise(0)
         prod[1] = keep.tile([P, PACK, HALF], BF16, name="prod1", tag="woven0", align_bytes=64)
-        for t in range(PACK):
-            weigh(t, 1)
+        nc.vector.tensor_tensor(prod[1][:], x_sb[1][:], gm_sb[:, :, cols(1)], MULT)
 
         scaled = {0: keep.tile([P, PACK, HALF], F32, name="scaled0", tag="w2_raw")}
 

@@ -90,7 +90,7 @@ def tile_list_toll_class_page_kernel(
                 nc.sync.dma_start(dst[32 * Q:32 * Q + 32], src)
 
         wgs_raw = [keep.tile([P, S], F32, name=f"wgs_raw{t}", tag=f"h{t}") for t in range(PACK)]
-        gained = keep.tile([P, PACK, S], F32, name="gained")
+        gained = keep.tile([P, PACK, S], F32, name="gained", tag="gained")
         wgs_rows = wgs.rearrange("(q t) j -> q t j", t=PACK)
         page0_sb = [keep.tile([P, T2], F32, name=f"page0_{t}") for t in range(PACK)]
 
@@ -106,12 +106,12 @@ def tile_list_toll_class_page_kernel(
         nc.sync.dma_start(idx3[:], offs3)
         load_dealt(wgs_raw[2][:], wgs_rows[:, 2, :])
         nc.sync.dma_start(page0_sb[2][:], rows_of(page0, 2))
-        gm_sb = keep.tile([P, PACK, S], F32, name="gm_sb")
-        nc.sync.dma_start(gm_sb[:], gm.rearrange("(p t) j -> p t j", t=PACK))
         load_dealt(wgs_raw[3][:], wgs_rows[:, 3, :])
         nc.sync.dma_start(page0_sb[3][:], rows_of(page0, 3))
         w2_raw = keep.tile([P, PACK, H], F32, name="w2_raw", tag="w2_raw")
         nc.sync.dma_start(w2_raw[:], w2.rearrange("(p j) n -> p j n", j=PACK))
+        gm_sb = keep.tile([P, PACK, S], F32, name="gm_sb")
+        nc.sync.dma_start(gm_sb[:], gm.rearrange("(p t) j -> p t j", t=PACK))
         nc.sync.dma_start(idx4[:], offs4)
 
         picked_sc = keep.tile([P, S], U8, name="picked_sc", align_bytes=64)
@@ -183,15 +183,17 @@ def tile_list_toll_class_page_kernel(
 
         x_sb = {}
         prod = {0: keep.tile([P, PACK, HALF], BF16, name="prod0", tag="prod0", align_bytes=64)}
-        woven = {0: keep.tile([P, HALF, PACK], BF16, name="woven0", tag="woven0", align_bytes=64)}
-        x_codes = {0: keep.tile([P, HALF], U32, name="x_codes0", align_bytes=64)}
-        x_planes = [keep.tile([P, HALF], U8, name=f"x_planes{h}", align_bytes=64) for h in range(2)]
+        both_woven = keep.tile([P, H + HALF, PACK], BF16, name="both_woven", tag="woven0", align_bytes=64)
+        both_codes = keep.tile([P, H + HALF], U32, name="both_codes", align_bytes=64)
+        both_planes = keep.tile([P, H + HALF], U8, name="both_planes", align_bytes=64)
+        woven = {0: both_woven[:, H:H + HALF, :]}
+        x_codes = {0: both_codes[:, H:H + HALF]}
+        x_planes = {0: both_planes[:, H:H + HALF]}
+        w2_codes = both_codes[:, 0:H]
+        w2_planes = both_planes[:, 0:H]
 
         def recall(t, h):
             nc.vector.tensor_copy(x_sb[h][:, t, :], page0_sb[t][:].indirect(list_half(idx3, h)))
-
-        def weigh(t, h):
-            nc.vector.tensor_tensor(prod[h][:, t, :], x_sb[h][:, t, :], gm_sb[:, t, cols(h)], MULT)
 
         def weave(h, pieces):
             width = HALF // pieces
@@ -201,44 +203,28 @@ def tile_list_toll_class_page_kernel(
                     prod[h][:, :, n * width:(n + 1) * width].rearrange("p t j -> p j t"),
                 )
 
-        def quantise(h):
-            nc.vector.quantize_mx(
-                out=x_codes[h][:].bitcast(FP8X4), scales=x_planes[h][:],
-                in_=woven[h][:].rearrange("p j t -> p (j t)"),
-            )
-
-        w2_woven = keep.tile([P, PACK * H], BF16, name="w2_woven", align_bytes=64)
-        w2_codes = keep.tile([P, H], U32, name="w2_codes", align_bytes=64)
-        w2_planes = keep.tile([P, H], U8, name="w2_planes", align_bytes=64)
-
-        x_sb[0] = keep.tile([P, PACK, HALF], F32, name="x_first", tag="x_first")
         first_product(0)
         put_states(0, 0)
         put_states(0, 1)
-        first_product(1)
-        put_states(1, None)
-        recall(0, 0)
-        first_product(2)
-        put_states(2, None)
-        recall(1, 0)
-        weigh(0, 0)
-        first_product(3)
+        for t in range(1, PACK):
+            first_product(t)
+            put_states(t, None)
         nc.scalar.copy(
-            w2_woven[:].rearrange("p (t m j) -> p t m j", t=PACK, j=PACK),
+            both_woven[:, 0:H, :].rearrange("p (t m) j -> p t m j", t=PACK),
             w2_raw[:].rearrange("p j (m t) -> p t m j", t=PACK),
         )
-        put_states(3, None)
+        x_sb[0] = keep.tile([P, PACK, HALF], F32, name="x_first", tag="gained")
         x_sb[1] = keep.tile([P, PACK, HALF], F32, name="x_second", tag="h3")
-        recall(2, 0)
-        weigh(1, 0)
-        recall(3, 0)
-        weigh(2, 0)
-        nc.vector.quantize_mx(out=w2_codes[:].bitcast(FP8X4), scales=w2_planes[:], in_=w2_woven[:])
-        weigh(3, 0)
+        for t in range(PACK):
+            recall(t, 0)
+            nc.gpsimd.tensor_tensor(prod[0][:, t, :], x_sb[0][:, t, :], gm_sb[:, t, cols(0)], MULT)
         weave(0, 1)
         for t in range(PACK):
             recall(t, 1)
-        quantise(0)
+        nc.vector.quantize_mx(
+            out=both_codes[:].bitcast(FP8X4), scales=both_planes[:],
+            in_=both_woven[:].rearrange("p j t -> p (j t)"),
+        )
         prod[1] = keep.tile([P, PACK, HALF], BF16, name="prod1", tag="woven0", align_bytes=64)
         nc.vector.tensor_tensor(prod[1][:], x_sb[1][:], gm_sb[:, :, cols(1)], MULT)
 
@@ -250,8 +236,8 @@ def tile_list_toll_class_page_kernel(
                 out=acc[:],
                 lhsT=w2_codes[:, t * P:(t + 1) * P].bitcast(FP8X4),
                 lhsT_scale=w2_planes[:, t * P:(t + 1) * P],
-                rhs=x_codes[h][:].bitcast(FP8X4),
-                rhs_scale=x_planes[h][:],
+                rhs=x_codes[h].bitcast(FP8X4),
+                rhs_scale=x_planes[h],
                 start=True,
                 stop=True,
             )
@@ -291,14 +277,21 @@ def tile_list_toll_class_page_kernel(
 
         put_result(0, 0, sum_on_vector(0, 0))
         y = sum_on_tensor(1, 0, keep.tile([P, HALF], F32, name="y_held", tag="held", align_bytes=64))
-        woven[1] = keep.tile([P, HALF, PACK], BF16, name="woven1", tag="prod0", align_bytes=64)
+        woven_second = keep.tile([P, HALF, PACK], BF16, name="woven_second", tag="prod0", align_bytes=64)
+        woven[1] = woven_second[:]
         weave(1, 4)
         put_result(1, 0, y)
-        x_codes[1] = keep.tile([P, HALF], U32, name="x_codes1", tag="held", align_bytes=64)
-        quantise(1)
+        codes_second = keep.tile([P, HALF], U32, name="codes_second", tag="held", align_bytes=64)
+        planes_second = keep.tile([P, HALF], U8, name="planes_second", align_bytes=64)
+        x_codes[1] = codes_second[:]
+        x_planes[1] = planes_second[:]
+        nc.vector.quantize_mx(
+            out=codes_second[:].bitcast(FP8X4), scales=planes_second[:],
+            in_=woven_second[:].rearrange("p j t -> p (j t)"),
+        )
         for t in range(2, PACK):
             put_result(t, 0, sum_on_tensor(t, 0))
-        scaled[1] = keep.tile([P, PACK, HALF], F32, name="scaled1", tag="x_first")
+        scaled[1] = keep.tile([P, PACK, HALF], F32, name="scaled1", tag="gained")
         for t in range(PACK):
             put_result(t, 1, sum_on_tensor(t, 1))
             nc.sync.dma_start(rows_of(out, t), page1_sb[t][:])

from contextlib import ExitStack

import concourse.mybir as mybir
from concourse.masks import make_identity

K, H, T, S, T2 = 1536, 512, 4096, 1024, 2048
FLOPS = 2 * K * H * S + 2 * H * H * S

F32 = mybir.dt.float32
BF16 = mybir.dt.bfloat16
I32 = mybir.dt.int32
U32 = mybir.dt.uint32
U16 = mybir.dt.uint16
U8 = mybir.dt.uint8
FP8X4 = mybir.dt.float8_e4m3fn_x4
FP4X4 = mybir.dt.float4_e2m1fn_x4
ACT = mybir.ActivationFunctionType
MULT = mybir.AluOpType.mult
ADD = mybir.AluOpType.add

P = 128
PACK = 4
PASSES = K // (P * PACK)
HALF = S // 2
LIST_COLS = S // 16
ROWS = 16 * PASSES
ROW0 = 48
PLANE = S + H


def tile_list_toll_class_page_kernel(
    tc, tab_words, tab_scales, offs, offs2, offs3, offs4, w4_words, w4_scales,
    gain, wgs, page0, gm, w2, back, wgo, page1, out,
):
    nc = tc.nc
    with ExitStack() as ctx:
        lists = ctx.enter_context(tc.tile_pool(name="lists", bufs=1))
        keep = ctx.enter_context(tc.tile_pool(name="keep", bufs=1))
        psum = ctx.enter_context(tc.psum_pool(name="psum", bufs=1))

        def cols(h):
            return slice(h * HALF, (h + 1) * HALF)

        def list_half(tile, h):
            return tile[:, h * LIST_COLS // 2:(h + 1) * LIST_COLS // 2]

        def rows_of(ap, t):
            return ap.rearrange("(p t) c -> p t c", t=PACK)[:, t, :]

        idx1 = lists.tile([P, LIST_COLS], U16, name="idx1")
        idx2 = lists.tile([P, LIST_COLS], U16, name="idx2")
        idx3 = lists.tile([P, LIST_COLS], U16, name="idx3")
        idx4 = lists.tile([P, LIST_COLS], U16, name="idx4")

        tab_sc = keep.tile([P, T], U8, name="tab_sc", align_bytes=64)
        w4_sc = keep.tile([P, H], U8, name="w4_sc", align_bytes=64)
        for tile in (tab_sc, w4_sc):
            nc.vector.memset(tile[0:ROW0, :].bitcast(I32), 0)
            nc.vector.memset(tile[ROW0 + ROWS:P, :].bitcast(I32), 0)
        planes = keep.tile([P, PASSES * PLANE], U8, name="planes", align_bytes=64)
        nc.gpsimd.memset(planes[:].bitcast(I32), 0)
        gain_sb = keep.tile([P, PACK], F32, name="gain_sb")
        nc.gpsimd.dma_start(gain_sb[:], gain.rearrange("(p t) -> p t", t=PACK))
        back_sb = keep.tile([P, PACK], F32, name="back_sb")
        nc.gpsimd.dma_start(back_sb[:], back.rearrange("(p t) -> p t", t=PACK))
        ident = keep.tile([P, P], F32, name="ident")
        make_identity(nc, ident[:])

        nc.sync.dma_start(idx1[:], offs)
        for tile, rows in ((tab_sc, tab_scales), (w4_sc, w4_scales)):
            nc.scalar.dma_start(
                tile[ROW0:ROW0 + ROWS, :].bitcast(I32),
                rows.bitcast(I32).rearrange("a q w -> q a w"),
            )
        w4_raw = keep.tile([P, PASSES * 2 * H], U8, name="w4_raw", align_bytes=64)
        nc.scalar.dma_start(
            w4_raw[:].bitcast(I32).rearrange("p (a w) -> p a w", a=PASSES),
            w4_words.bitcast(I32).rearrange("a p w -> p a w"),
        )
        tab_w = [keep.tile([P, T], U32, name=f"tab_w{a}", tag="big", bufs=3, align_bytes=64) for a in range(PASSES)]

        def load_tab(a):
            nc.sync.dma_start(
                tab_w[a][:].bitcast(I32),
                tab_words[a].rearrange("p t i -> p (t i)").bitcast(I32),
            )

        def load_dealt(dst, src):
            for Q in (0, 2, 1, 3):
                nc.sync.dma_start(dst[32 * Q:32 * Q + 32], src)

        wgs_raw = [keep.tile([P, S], F32, name=f"wgs_raw{t}", tag=f"h{t}") for t in range(PACK)]
        gained = keep.tile([P, PACK, S], F32, name="gained", tag="gained")
        wgs_rows = wgs.rearrange("(q t) j -> q t j", t=PACK)
        page0_sb = [keep.tile([P, T2], F32, name=f"page0_{t}") for t in range(PACK)]

        load_tab(0)
        load_tab(1)
        load_tab(2)
        nc.sync.dma_start(idx2[:], offs2)
        load_dealt(wgs_raw[0][:, cols(0)], wgs_rows[:, 0, cols(0)])
        nc.sync.dma_start(page0_sb[0][:], rows_of(page0, 0))
        load_dealt(wgs_raw[0][:, cols(1)], wgs_rows[:, 0, cols(1)])
        load_dealt(wgs_raw[1][:], wgs_rows[:, 1, :])
        nc.sync.dma_start(page0_sb[1][:], rows_of(page0, 1))
        nc.sync.dma_start(idx3[:], offs3)
        load_dealt(wgs_raw[2][:], wgs_rows[:, 2, :])
        nc.sync.dma_start(page0_sb[2][:], rows_of(page0, 2))
        load_dealt(wgs_raw[3][:], wgs_rows[:, 3, :])
        nc.sync.dma_start(page0_sb[3][:], rows_of(page0, 3))
        w2_raw = keep.tile([P, PACK, H], F32, name="w2_raw", tag="w2_raw")
        nc.sync.dma_start(w2_raw[:], w2.rearrange("(p j) n -> p j n", j=PACK))
        gm_sb = keep.tile([P, PACK, S], F32, name="gm_sb")
        nc.sync.dma_start(gm_sb[:], gm.rearrange("(p t) j -> p t j", t=PACK))
        nc.sync.dma_start(idx4[:], offs4)

        picked_sc = keep.tile([P, S], U8, name="picked_sc", align_bytes=64)
        nc.vector.tensor_copy(picked_sc[:], tab_sc[:].indirect(idx1[:]))
        staged = keep.tile([P, PLANE], U8, name="staged", align_bytes=64)
        nc.vector.tensor_copy(
            staged[:, S:PLANE].rearrange("p (t q) -> p t q", t=PACK),
            w4_sc[:].rearrange("p (q t) -> p t q", t=PACK),
        )
        nc.vector.tensor_copy(staged[:, 0:S].bitcast(I32), picked_sc[:].bitcast(I32))
        for Q in range(4):
            first = ROW0 + 4 * PASSES * Q
            nc.gpsimd.dma_start(
                planes[32 * Q:32 * Q + 4, :].bitcast(I32),
                staged[first:first + 4 * PASSES, :].bitcast(I32),
            )
        w4_codes = keep.tile([P, PASSES * 2 * H], U8, name="w4_codes", align_bytes=64)
        nc.vector.tensor_copy(
            w4_codes[:].bitcast(U16).rearrange("p (a t q) -> p a t q", a=PASSES, t=PACK),
            w4_raw[:].bitcast(U16).rearrange("p (a q t) -> p a t q", a=PASSES, t=PACK),
        )
        v_words = [keep.tile([P, S], U32, name=f"v_words{a}", align_bytes=64) for a in range(PASSES)]
        nc.vector.tensor_copy(v_words[0][:], tab_w[0][:].indirect(idx1[:]))
        nc.vector.tensor_copy(v_words[1][:], tab_w[1][:].indirect(idx1[:]))
        for h in range(2):
            nc.vector.tensor_copy(v_words[2][:, cols(h)], tab_w[2][:].indirect(list_half(idx1, h)))

        wgo_sb = keep.tile([P, PACK, S], F32, name="wgo_sb", tag="big", bufs=3, align_bytes=64)
        page1_sb = [keep.tile([P, T2], F32, name=f"page1_{t}", tag="big", bufs=3, align_bytes=64) for t in range(2)]
        page1_sb.extend([keep.tile([P, T2], F32, name=f"page1_{t}") for t in range(2, PACK)])
        wgo_rows = wgo.rearrange("(q t) j -> q t j", t=PACK)
        load_dealt(wgo_sb[:, :, cols(0)], wgo_rows[:, :, cols(0)])
        for t in range(PACK):
            nc.sync.dma_start(page1_sb[t][:], rows_of(page1, t))
        load_dealt(wgo_sb[:, :, cols(1)], wgo_rows[:, :, cols(1)])

        h_sb = []

        def first_product(t):
            if t == 0:
                for h in range(2):
                    nc.scalar.activation(
                        gained[:, t, cols(h)], wgs_raw[t][:, cols(h)], ACT.Copy, scale=gain_sb[:, t:t + 1])
                ht = keep.tile([P, S], F32, name="h_first")
            else:
                nc.scalar.activation(gained[:, t, :], wgs_raw[t][:], ACT.Copy, scale=gain_sb[:, t:t + 1])
                ht = keep.tile([P, S], F32, name=f"h{t}", tag=f"h{t}")
            for h in range(2):
                acc = psum.tile([P, HALF], F32, name="acc1", tag="acc1", bufs=2)
                for a in range(PASSES):
                    nc.tensor.matmul_mx(
                        out=acc[:],
                        lhsT=w4_codes[:, (a * PACK + t) * 2 * P:(a * PACK + t + 1) * 2 * P].bitcast(FP4X4),
                        lhsT_scale=planes[:, a * PLANE + S + t * P:a * PLANE + S + (t + 1) * P],
                        rhs=v_words[a][:, cols(h)].bitcast(FP8X4),
                        rhs_scale=planes[:, a * PLANE + h * HALF:a * PLANE + (h + 1) * HALF],
                        start=(a == 0),
                        stop=(a == PASSES - 1),
                    )
                nc.scalar.activation(ht[:, cols(h)], acc[:], ACT.Gelu_apprx_tanh)
            h_sb.append(ht)

        def put_states(t, h):
            if h is None:
                nc.vector.tensor_tensor(page0_sb[t][:].indirect(idx2[:]), h_sb[t][:], gained[:, t, :], MULT)
            else:
                nc.vector.tensor_tensor(
                    page0_sb[t][:].indirect(list_half(idx2, h)), h_sb[t][:, cols(h)], gained[:, t, cols(h)], MULT)

        x_sb = {}
        prod = {0: keep.tile([P, PACK, HALF], BF16, name="prod0", tag="prod0", align_bytes=64)}
        both_woven = keep.tile([P, H + HALF, PACK], BF16, name="both_woven", tag="woven0", align_bytes=64)
        both_codes = keep.tile([P, H + HALF], U32, name="both_codes", align_bytes=64)
        both_planes = keep.tile([P, H + HALF], U8, name="both_planes", align_bytes=64)
        woven = {0: both_woven[:, H:H + HALF, :]}
        x_codes = {0: both_codes[:, H:H + HALF]}
        x_planes = {0: both_planes[:, H:H + HALF]}
        w2_codes = both_codes[:, 0:H]
        w2_planes = both_planes[:, 0:H]

        def recall(t, h):
            nc.vector.tensor_copy(x_sb[h][:, t, :], page0_sb[t][:].indirect(list_half(idx3, h)))

        def weave(h, pieces):
            width = HALF // pieces
            for n in range(pieces):
                nc.scalar.copy(
                    woven[h][:, n * width:(n + 1) * width, :],
                    prod[h][:, :, n * width:(n + 1) * width].rearrange("p t j -> p j t"),
                )

        first_product(0)
        put_states(0, 0)
        put_states(0, 1)
        for t in range(1, PACK):
            first_product(t)
            put_states(t, None)
        nc.scalar.copy(
            both_woven[:, 0:H, :].rearrange("p (t m) j -> p t m j", t=PACK),
            w2_raw[:].rearrange("p j (m t) -> p t m j", t=PACK),
        )
        x_sb[0] = keep.tile([P, PACK, HALF], F32, name="x_first", tag="gained")
        x_sb[1] = keep.tile([P, PACK, HALF], F32, name="x_second", tag="h3")
        for t in range(PACK):
            recall(t, 0)
            nc.gpsimd.tensor_tensor(prod[0][:, t, :], x_sb[0][:, t, :], gm_sb[:, t, cols(0)], MULT)
        weave(0, 1)
        for t in range(PACK):
            recall(t, 1)
        nc.vector.quantize_mx(
            out=both_codes[:].bitcast(FP8X4), scales=both_planes[:],
            in_=both_woven[:].rearrange("p j t -> p (j t)"),
        )
        prod[1] = keep.tile([P, PACK, HALF], BF16, name="prod1", tag="woven0", align_bytes=64)
        nc.vector.tensor_tensor(prod[1][:], x_sb[1][:], gm_sb[:, :, cols(1)], MULT)

        scaled = {0: keep.tile([P, PACK, HALF], F32, name="scaled0", tag="w2_raw")}

        def second_product(t, h):
            acc = psum.tile([P, HALF], F32, name="acc2", tag="acc2", bufs=3)
            nc.tensor.matmul_mx(
                out=acc[:],
                lhsT=w2_codes[:, t * P:(t + 1) * P].bitcast(FP8X4),
                lhsT_scale=w2_planes[:, t * P:(t + 1) * P],
                rhs=x_codes[h].bitcast(FP8X4),
                rhs_scale=x_planes[h],
                start=True,
                stop=True,
            )
            mixed = keep.tile([P, HALF], F32, name="mixed", tag="mixed", bufs=2)
            nc.scalar.activation(mixed[:], acc[:], ACT.Tanh)
            return mixed

        def sum_on_vector(t, h):
            mixed = second_product(t, h)
            y = keep.tile([P, HALF], F32, name="y", tag="y", bufs=3)
            nc.vector.scalar_tensor_tensor(y[:], x_sb[h][:, t, :], back_sb[:, t:t + 1], mixed[:], MULT, ADD)
            return y

        def sum_on_tensor(t, h, y=None):
            blocks = HALF // P
            nc.scalar.activation(scaled[h][:, t, :], x_sb[h][:, t, :], ACT.Copy, scale=back_sb[:, t:t + 1])
            mixed = second_product(t, h)
            turned = psum.tile([P, HALF], F32, name="turned", tag="acc1", bufs=2)
            for n, term in enumerate((scaled[h][:, t, :], mixed[:])):
                for b in range(blocks):
                    nc.tensor.matmul(
                        turned[:, b * P:(b + 1) * P], lhsT=term[:, b * P:(b + 1) * P], rhs=ident[:],
                        is_transpose=True, start=(n == 0 and b == 0), stop=(n == 1 and b == blocks - 1),
                    )
            turned_sb = keep.tile([P, HALF], F32, name="turned_sb", tag="turned_sb", bufs=2)
            nc.scalar.copy(turned_sb[:], turned[:])
            upright = psum.tile([P, HALF], F32, name="upright", tag="upright", bufs=3)
            for b in range(blocks):
                nc.tensor.transpose(upright[:, b * P:(b + 1) * P], turned_sb[:, b * P:(b + 1) * P], ident[:])
            if y is None:
                y = keep.tile([P, HALF], F32, name="y", tag="y", bufs=3)
            nc.scalar.copy(y[:], upright[:])
            return y

        def put_result(t, h, y):
            nc.vector.tensor_tensor(page1_sb[t][:].indirect(list_half(idx4, h)), y[:], wgo_sb[:, t, cols(h)], MULT)

        put_result(0, 0, sum_on_vector(0, 0))
        y = sum_on_tensor(1, 0, keep.tile([P, HALF], F32, name="y_held", tag="held", align_bytes=64))
        woven_second = keep.tile([P, HALF, PACK], BF16, name="woven_second", tag="prod0", align_bytes=64)
        woven[1] = woven_second[:]
        weave(1, 4)
        put_result(1, 0, y)
        codes_second = keep.tile([P, HALF], U32, name="codes_second", tag="held", align_bytes=64)
        planes_second = keep.tile([P, HALF], U8, name="planes_second", align_bytes=64)
        x_codes[1] = codes_second[:]
        x_planes[1] = planes_second[:]
        nc.vector.quantize_mx(
            out=codes_second[:].bitcast(FP8X4), scales=planes_second[:],
            in_=woven_second[:].rearrange("p j t -> p (j t)"),
        )
        for t in range(2, PACK):
            put_result(t, 0, sum_on_tensor(t, 0))
        scaled[1] = keep.tile([P, PACK, HALF], F32, name="scaled1", tag="gained")
        for t in range(PACK):
            put_result(t, 1, sum_on_tensor(t, 1))
            nc.sync.dma_start(rows_of(out, t), page1_sb[t][:])
